import numpy as np
import ml_dtypes


def mxq(x, axis, fmt="e4m3"):
    dtype, down = {"e4m3": (ml_dtypes.float8_e4m3fn, 7), "e5m2": (ml_dtypes.float8_e5m2, 14)}[fmt]
    v = np.moveaxis(np.asarray(x, np.float32).astype(ml_dtypes.bfloat16).astype(np.float64), axis, -1)
    blocks = v.reshape(v.shape[:-1] + (-1, 32))
    amax = np.abs(blocks).max(-1, keepdims=True)
    byte = np.maximum(np.where(amax > 0, np.frexp(amax)[1] - 1 + 127, 0) - down, 1)
    scale = np.exp2(byte - 127.0)
    codes = (blocks / scale).astype(np.float32).astype(dtype).astype(np.float64)
    return np.moveaxis((codes * scale).reshape(v.shape), -1, axis)


WIDE = False


def mx_kscale(k):
    if not WIDE:
        return np.ones(k)
    levels = np.array([10, -10, 5, -5, 0])
    if k % 512:
        return np.exp2(np.random.permutation(np.resize(levels, k // 32))).repeat(32)
    a = np.empty((k // 512, 16))
    for p in range(k // 512):
        a[p, :8] = np.random.permutation(np.resize(levels, 8))
        for g in range(8):
            far = levels[np.abs(levels - a[p, g]) >= 10]
            a[p, g + 8] = far[np.random.randint(len(far))]
    return np.exp2(a.ravel()).repeat(32)


BF16 = ml_dtypes.bfloat16


def bf(x):
    return np.asarray(x, np.float32).astype(BF16)


def f64(x):
    return np.asarray(x).astype(np.float64)


N, F, H, K, C = 1024, 16, 512, 128, 512
FK = F * K


def draw0():
    t = mx_kscale(H)
    r = mx_kscale(FK)
    return {
        "x": bf(np.random.standard_normal((N, F))),
        "a": bf(np.random.standard_normal(H)),
        "b": bf(np.random.standard_normal(H) * 0.5),
        "g": bf(np.random.standard_normal(H) * t),
        "w": bf(np.random.standard_normal((H, K)) * (2.0 / np.sqrt(H)) / t[:, None]),
        "s": bf(np.random.standard_normal((F, K)) * r.reshape(F, K)),
        "v": bf(np.random.standard_normal((FK, C)) / np.sqrt(FK) / r[:, None]),
    }


def shared_basis(x, a, b, g, w):
    u = np.maximum(a * x[:, :, None] + b, 0.0) * g
    z = mxq(u, 2, "e4m3") @ mxq(w, 0, "e4m3")
    return np.maximum(z, 0.0)


def core(x, a, b, g, w, s, v):
    z = shared_basis(f64(x), f64(a), f64(b), f64(g), f64(w))
    q = (z * f64(s)[None, :, :]).reshape(x.shape[0], v.shape[0])
    return mxq(q, 1, "e4m3") @ mxq(f64(v), 0, "e4m3")


def e4m3fn_bytes(y):
    return np.clip(np.asarray(y, np.float64), -448.0, 448.0).astype(np.float32).astype(ml_dtypes.float8_e4m3fn).view(np.uint8)


def e4m3fn_values(b):
    return np.asarray(b, np.uint8).view(ml_dtypes.float8_e4m3fn).astype(np.float64)


def setup_inputs():
    d = draw0()
    x0 = np.asarray(d['v']).astype(np.float64)
    s = (np.max(np.abs(x0), axis=(1,), keepdims=True) / 448.0).astype(np.float32)
    out = {}
    for k, v in d.items():
        if k == 'v':
            out['v_bytes'] = e4m3fn_bytes(x0 / s.astype(np.float64))
            out['v_scale'] = s
        else:
            out[k] = v
    return out


def reference(x, a, b, g, w, s, v_bytes, v_scale):
    return core(x, a, b, g, w, s, e4m3fn_values(v_bytes) * v_scale.astype(np.float64))

@@ -1,0 +1,263 @@
+from contextlib import ExitStack
+
+import concourse.mybir as mybir
+from concourse.masks import make_identity
+
+N, F, H, K, C = 1024, 16, 512, 128, 512
+FLOPS = 2 * N * F * H * K + 2 * N * F * K * C
+
+F32 = mybir.dt.float32
+BF16 = mybir.dt.bfloat16
+U32 = mybir.dt.uint32
+U8 = mybir.dt.uint8
+FP8 = mybir.dt.float8_e4m3fn
+FP8X4 = mybir.dt.float8_e4m3fn_x4
+ALU = mybir.AluOpType
+ACT = mybir.ActivationFunctionType
+
+P = 128
+PACK = 4
+TILES = N // P
+GROUPS = F // PACK
+UNITS = TILES * GROUPS
+UNIT_COLS = PACK * P
+QUAD = 32
+GAP = P - QUAD
+RUN = 4
+VECTOR_COLS = 432
+LAST_COLS = 288
+
+
+def tile_neuralbasismodelsharedshapes_kernel(tc, x, a, b, g, w, s, v_bytes, v_scale, out):
+    nc = tc.nc
+    with ExitStack() as ctx:
+        keep = ctx.enter_context(tc.tile_pool(name="keep", bufs=1))
+        work = ctx.enter_context(tc.tile_pool(name="work", bufs=2))
+        psum = ctx.enter_context(tc.psum_pool(name="psum", bufs=1))
+        ctx.enter_context(tc.manual_schedule())
+
+        x_rows = keep.tile([P, TILES * F], BF16, name="x_rows")
+        nc.sync.dma_start(out=x_rows[:], in_=x.rearrange("(p j) f -> p (j f)", j=TILES))
+        a_sb = keep.tile([P, PACK], BF16, name="a_sb")
+        b_sb = keep.tile([P, PACK], BF16, name="b_sb")
+        g_sb = keep.tile([P, PACK], BF16, name="g_sb")
+        for dst, src in ((g_sb, g), (a_sb, a), (b_sb, b)):
+            nc.scalar.dma_start(out=dst[:], in_=src.rearrange("(p t) -> p t", t=PACK))
+        vs_sb = keep.tile([P, GROUPS, PACK], F32, name="vs_sb")
+        nc.sync.dma_start(out=vs_sb[:], in_=v_scale.rearrange("(q p t) o -> p q (t o)", p=P, t=PACK))
+        v_view = v_bytes.rearrange("(q p t) c -> q p t c", p=P, t=PACK)
+        v_raw = [keep.tile([P, PACK, C], U8, name="v_raw%d" % q) for q in range(GROUPS)]
+        nc.sync.dma_start(out=v_raw[0][:], in_=v_view[0])
+        w_sb = keep.tile([P, PACK, K], BF16, name="w_sb")
+        nc.sync.dma_start(out=w_sb[:], in_=w.rearrange("(p t) k -> p t k", t=PACK))
+        nc.sync.dma_start(out=v_raw[1][:], in_=v_view[1])
+        nc.sync.dma_start(out=v_raw[2][:], in_=v_view[2])
+        s_sb = keep.tile([P, GROUPS, PACK], BF16, name="s_sb")
+        nc.scalar.dma_start(out=s_sb[:], in_=s.rearrange("f k -> (f k)").rearrange("(q p t) -> p q t", p=P, t=PACK))
+
+        ident = keep.tile([P, P], BF16, name="ident")
+        make_identity(nc, ident[:])
+        w_pad = keep.tile([P, GAP + PACK * P], U32, name="w_pad", align_bytes=64)
+        nc.vector.memset(w_pad[:], 0)
+        xt_ps = psum.tile([P, P], BF16, name="xt_ps", tag="acc", bufs=2)
+        nc.tensor.transpose(xt_ps[:], x_rows[:], ident[:])
+        xt_sb = keep.tile([P, P], BF16, name="xt_sb")
+        nc.vector.tensor_copy(out=xt_sb[:], in_=xt_ps[:])
+        parked = out[0:F, :].rearrange("r c -> (r c)")
+        nc.scalar.dma_start(out=parked.rearrange("(p n) -> p n", p=P), in_=xt_sb[:].bitcast(F32))
+        x_all = [keep.tile([P, F * P], BF16, name="x_all%d" % j) for j in range(TILES)]
+        tile_words = F * P // 2
+
+        def spread_x(j):
+            words = parked[j * tile_words : (j + 1) * tile_words]
+            nc.sync.dma_start(out=x_all[j][:].bitcast(F32), in_=words.partition_broadcast(P))
+
+        spread_x(0)
+        nc.sync.dma_start(out=v_raw[3][:], in_=v_view[3])
+        for j in range(1, TILES):
+            spread_x(j)
+
+        sign2 = keep.tile([P, PACK], F32, name="sign2")
+        nc.vector.tensor_scalar(out=sign2[:], in0=g_sb[:], scalar1=0.0, scalar2=2.0, op0=ALU.is_ge, op1=ALU.mult)
+        sign = keep.tile([P, PACK], F32, name="sign")
+        nc.vector.tensor_scalar(out=sign[:], in0=sign2[:], scalar1=-1.0, scalar2=None, op0=ALU.add)
+        g_abs = keep.tile([P, PACK], F32, name="g_abs")
+        nc.vector.tensor_tensor(out=g_abs[:], in0=g_sb[:], in1=sign[:], op=ALU.mult)
+        w_rep = keep.tile([P, PACK, PACK, QUAD * PACK], BF16, name="w_rep", align_bytes=64)
+        nc.vector.tensor_tensor(
+            out=w_rep[:, :, 0, :].rearrange("p e (m t) -> p e m t", t=PACK),
+            in0=w_sb[:].rearrange("p t (m e) -> p e m t", e=PACK),
+            in1=sign[:].unsqueeze(1).unsqueeze(1).to_broadcast([P, PACK, QUAD, PACK]),
+            op=ALU.mult,
+        )
+        slope = keep.tile([P, PACK], F32, name="slope")
+        nc.vector.tensor_tensor(out=slope[:], in0=a_sb[:], in1=g_abs[:], op=ALU.mult)
+        shift = keep.tile([P, PACK], F32, name="shift")
+        nc.vector.tensor_tensor(out=shift[:], in0=b_sb[:], in1=g_abs[:], op=ALU.mult)
+        nc.vector.tensor_copy(
+            out=w_rep[:, :, 1:PACK, :],
+            in_=w_rep[:, :, 0:1, :].to_broadcast([P, PACK, PACK - 1, QUAD * PACK]),
+        )
+        s32 = keep.tile([P, GROUPS, PACK], F32, name="s32")
+        nc.vector.tensor_copy(out=s32[:], in_=s_sb[:])
+        w_codes = keep.tile([P, PACK, P], U32, name="w_codes", align_bytes=64)
+        w_scales = keep.tile([P, PACK, P], U8, name="w_scales", align_bytes=64)
+        nc.vector.quantize_mx(
+            out=w_codes[:].rearrange("p e c -> p (e c)").bitcast(FP8X4),
+            scales=w_scales[:].rearrange("p e c -> p (e c)"),
+            in_=w_rep[:].rearrange("p e r c -> p (e r c)"),
+        )
+
+        v_codes = keep.tile([P, GROUPS, C], U32, name="v_codes", align_bytes=64)
+        v_scales = keep.tile([P, GROUPS, C], U8, name="v_scales", align_bytes=64)
+        v_planes, v_grouped = {}, {}
+        planes, u_grouped, u_mx, z_ps, q_grouped, q_mx, acc = {}, {}, {}, {}, {}, {}, {}
+
+        def run_views(dst, src):
+            return (
+                dst.rearrange("p (c i) t -> p c t i", i=RUN),
+                src.rearrange("p t (c i) -> p c t i", i=RUN),
+            )
+
+        def widen_v(q):
+            v_planes[q] = work.tile([P, PACK, C], BF16, name="v_planes", bufs=GROUPS)
+            for t in range(PACK):
+                nc.scalar.activation(
+                    out=v_planes[q][:, t, :], in_=v_raw[q][:, t, :].bitcast(FP8), func=ACT.Copy, scale=vs_sb[:, q, t : t + 1]
+                )
+
+        def group_v(q):
+            v_grouped[q] = work.tile([P, C, PACK], BF16, name="v_grouped", align_bytes=64)
+            dst, src = run_views(v_grouped[q][:], v_planes[q][:])
+            nc.vector.tensor_copy(out=dst, in_=src)
+
+        def quantize_v(q):
+            nc.vector.quantize_mx(
+                out=v_codes[:, q, :].bitcast(FP8X4), scales=v_scales[:, q, :], in_=v_grouped[q][:].rearrange("p c t -> p (c t)")
+            )
+
+        def affine(j, t):
+            if j not in planes:
+                planes[j] = work.tile([P, PACK, F * P], BF16, name="planes", bufs=3)
+            nc.vector.tensor_scalar(
+                out=planes[j][:, t, :], in0=x_all[j][:], scalar1=slope[:, t : t + 1], scalar2=shift[:, t : t + 1], op0=ALU.mult, op1=ALU.add
+            )
+
+        def relu_views(u, c0, c1):
+            j, q = divmod(u, GROUPS)
+            if u not in u_grouped:
+                u_grouped[u] = work.tile([P, UNIT_COLS, PACK], BF16, name="u_grouped", bufs=4, align_bytes=64)
+            return run_views(u_grouped[u][:, c0:c1, :], planes[j][:, :, q * UNIT_COLS + c0 : q * UNIT_COLS + c1])
+
+        def vector_share(u):
+            if u >= UNITS - 2:
+                return LAST_COLS
+            return VECTOR_COLS if u % GROUPS == 0 else 0
+
+        def relu_scalar(u):
+            dst, src = relu_views(u, vector_share(u), UNIT_COLS)
+            nc.scalar.activation(out=dst, in_=src, func=ACT.Relu)
+
+        def relu_vector(u):
+            dst, src = relu_views(u, 0, vector_share(u))
+            nc.vector.tensor_scalar(out=dst, in0=src, scalar1=0.0, scalar2=None, op0=ALU.max)
+
+        def quantize_u(u):
+            codes = work.tile([P, UNIT_COLS], U32, name="u_codes", bufs=3, align_bytes=64)
+            scales = work.tile([P, UNIT_COLS], U8, name="u_scales", bufs=3, align_bytes=64)
+            u_mx[u] = (codes, scales)
+            nc.vector.quantize_mx(out=codes[:].bitcast(FP8X4), scales=scales[:], in_=u_grouped[u][:].rearrange("p c t -> p (c t)"))
+
+        def first_matmul(u):
+            codes, scales = u_mx[u]
+            z_ps[u] = psum.tile([P, PACK, P], F32, name="z_ps", tag="z", bufs=4)
+            for e in range(PACK):
+                for l in range(PACK):
+                    w0 = GAP + e * P - l * QUAD
+                    nc.tensor.matmul_mx(
+                        out=z_ps[u][:, e, :],
+                        lhsT=w_pad[:, w0 : w0 + P].bitcast(FP8X4),
+                        lhsT_scale=w_scales[:, e, :],
+                        rhs=codes[:, l * P : (l + 1) * P].bitcast(FP8X4),
+                        rhs_scale=scales[:, l * P : (l + 1) * P],
+                        start=(l == 0),
+                        stop=(l == PACK - 1),
+                    )
+
+        def make_q(u):
+            q = u % GROUPS
+            q_grouped[u] = work.tile([P, P, PACK], BF16, name="q_grouped", bufs=3, align_bytes=64)
+            nc.vector.scalar_tensor_tensor(
+                out=q_grouped[u][:],
+                in0=z_ps[u][:].rearrange("p e n -> p n e"),
+                scalar=0.0,
+                in1=s32[:, q : q + 1, :].to_broadcast([P, P, PACK]),
+                op0=ALU.max,
+                op1=ALU.mult,
+            )
+
+        def quantize_q(u):
+            codes = work.tile([P, P], U32, name="q_codes", bufs=3, align_bytes=64)
+            scales = work.tile([P, P], U8, name="q_scales", bufs=3, align_bytes=64)
+            q_mx[u] = (codes, scales)
+            nc.vector.quantize_mx(out=codes[:].bitcast(FP8X4), scales=scales[:], in_=q_grouped[u][:].rearrange("p n t -> p (n t)"))
+
+        def second_matmul(u):
+            j, q = divmod(u, GROUPS)
+            codes, scales = q_mx[u]
+            if q == 0:
+                acc[j] = psum.tile([P, C], F32, name="acc", tag="acc", bufs=2)
+            nc.tensor.matmul_mx(
+                out=acc[j][:],
+                lhsT=codes[:].bitcast(FP8X4),
+                lhsT_scale=scales[:],
+                rhs=v_codes[:, q, :].bitcast(FP8X4),
+                rhs_scale=v_scales[:, q, :],
+                start=(q == 0),
+                stop=(q == GROUPS - 1),
+            )
+
+        out_tiles = out.rearrange("(p j) c -> j p c", j=TILES)
+
+        def store(j):
+            result = work.tile([P, C], F32, name="result", bufs=TILES)
+            nc.scalar.copy(out=result[:], in_=acc[j][:])
+            nc.sync.dma_start(out=out_tiles[j], in_=result[:])
+
+        for q in range(GROUPS):
+            widen_v(q)
+        group_v(0)
+        nc.vector.tensor_copy(
+            out=w_pad[:, GAP:].rearrange("p (e c) -> p e c", e=PACK)[:, :, 0:QUAD].bitcast(U8),
+            in_=w_codes[:, :, 0:QUAD].bitcast(U8),
+        )
+        group_v(1)
+        quantize_v(0)
+        group_v(2)
+        quantize_v(1)
+        for t in range(PACK):
+            affine(0, t)
+
+        for step in range(UNITS + 5):
+            j, q = divmod(step, GROUPS)
+            if step < UNITS:
+                relu_scalar(step)
+                if vector_share(step):
+                    relu_vector(step)
+            if step == 0:
+                quantize_v(2)
+                group_v(3)
+            if step == 1:
+                quantize_v(3)
+            if 0 <= step - 1 < UNITS:
+                quantize_u(step - 1)
+                first_matmul(step - 1)
+            if j + 1 < TILES:
+                affine(j + 1, q)
+            if 0 <= step - 3 < UNITS:
+                quantize_q(step - 3)
+                second_matmul(step - 3)
+            if 0 <= step - 2 < UNITS:
+                make_q(step - 2)
+            if step >= 7 and (step - 7) % GROUPS == 0 and (step - 7) // GROUPS < TILES:
+                store((step - 7) // GROUPS)

@@ -24,8 +24,12 @@ UNIT_COLS = PACK * P
 QUAD = 32
 GAP = P - QUAD
 RUN = 4
-VECTOR_COLS = 432
-LAST_COLS = 288
+VECTOR_COLS = 160
+LAST_COLS = (0, 0, 128, 256)
+FIRST_COLS = (512, 512)
+GPSIMD_COLS = 320
+BIG = 3.3895313892515355e38
+FIRST_GP = 128
 
 
 def tile_neuralbasismodelsharedshapes_kernel(tc, x, a, b, g, w, s, v_bytes, v_scale, out):
@@ -38,11 +42,11 @@ def tile_neuralbasismodelsharedshapes_kernel(tc, x, a, b, g, w, s, v_bytes, v_sc
 
         x_rows = keep.tile([P, TILES * F], BF16, name="x_rows")
         nc.sync.dma_start(out=x_rows[:], in_=x.rearrange("(p j) f -> p (j f)", j=TILES))
-        a_sb = keep.tile([P, PACK], BF16, name="a_sb")
-        b_sb = keep.tile([P, PACK], BF16, name="b_sb")
         g_sb = keep.tile([P, PACK], BF16, name="g_sb")
-        for dst, src in ((g_sb, g), (a_sb, a), (b_sb, b)):
-            nc.scalar.dma_start(out=dst[:], in_=src.rearrange("(p t) -> p t", t=PACK))
+        ab_sb = keep.tile([P, 2, 16], BF16, name="ab_sb")
+        nc.scalar.dma_start(out=g_sb[:], in_=g.rearrange("(p t) -> p t", t=PACK))
+        nc.scalar.dma_start(out=ab_sb[:, 0, 0:PACK], in_=a.rearrange("(p t) -> p t", t=PACK))
+        nc.scalar.dma_start(out=ab_sb[:, 1, 0:PACK], in_=b.rearrange("(p t) -> p t", t=PACK))
         vs_sb = keep.tile([P, GROUPS, PACK], F32, name="vs_sb")
         nc.sync.dma_start(out=vs_sb[:], in_=v_scale.rearrange("(q p t) o -> p q (t o)", p=P, t=PACK))
         v_view = v_bytes.rearrange("(q p t) c -> q p t c", p=P, t=PACK)
@@ -52,6 +56,7 @@ def tile_neuralbasismodelsharedshapes_kernel(tc, x, a, b, g, w, s, v_bytes, v_sc
         nc.sync.dma_start(out=w_sb[:], in_=w.rearrange("(p t) k -> p t k", t=PACK))
         nc.sync.dma_start(out=v_raw[1][:], in_=v_view[1])
         nc.sync.dma_start(out=v_raw[2][:], in_=v_view[2])
+        nc.sync.dma_start(out=v_raw[3][:], in_=v_view[3])
         s_sb = keep.tile([P, GROUPS, PACK], BF16, name="s_sb")
         nc.scalar.dma_start(out=s_sb[:], in_=s.rearrange("f k -> (f k)").rearrange("(q p t) -> p q t", p=P, t=PACK))
 
@@ -65,48 +70,62 @@ def tile_neuralbasismodelsharedshapes_kernel(tc, x, a, b, g, w, s, v_bytes, v_sc
         nc.vector.tensor_copy(out=xt_sb[:], in_=xt_ps[:])
         parked = out[0:F, :].rearrange("r c -> (r c)")
         nc.scalar.dma_start(out=parked.rearrange("(p n) -> p n", p=P), in_=xt_sb[:].bitcast(F32))
-        x_all = [keep.tile([P, F * P], BF16, name="x_all%d" % j) for j in range(TILES)]
-        tile_words = F * P // 2
-
-        def spread_x(j):
-            words = parked[j * tile_words : (j + 1) * tile_words]
-            nc.sync.dma_start(out=x_all[j][:].bitcast(F32), in_=words.partition_broadcast(P))
-
-        spread_x(0)
-        nc.sync.dma_start(out=v_raw[3][:], in_=v_view[3])
+        tile_cols = F * P
+        half = tile_cols // 2
+        x_all = {}
         for j in range(1, TILES):
-            spread_x(j)
+            x_all[j, 0] = keep.tile([P, tile_cols], BF16, name="x_all%d" % j)
+            words = parked[j * half : (j + 1) * half]
+            nc.sync.dma_start(out=x_all[j, 0][:].bitcast(F32), in_=words.partition_broadcast(P))
+        first_ps = {}
+        for c0 in (0, half):
+            first_ps[c0] = psum.tile([P, half], BF16, name="first_ps", tag="z", bufs=6)
+            for f in range(c0 // P, (c0 + half) // P):
+                nc.tensor.transpose(first_ps[c0][:, f * P - c0 : (f + 1) * P - c0], x_rows[:, f : f + 1].to_broadcast([P, P]), ident[:])
 
+        def fetch_first(c0):
+            x_all[0, c0] = keep.tile([P, half], BF16, name="x_first%d" % c0)
+            nc.scalar.copy(out=x_all[0, c0][:], in_=first_ps[c0][:])
+
+        g_abs = keep.tile([P, 1, PACK], F32, name="g_abs")
+        nc.vector.scalar_tensor_tensor(out=g_abs[:, 0, :], in0=g_sb[:], scalar=-1.0, in1=g_sb[:], op0=ALU.mult, op1=ALU.max)
         sign2 = keep.tile([P, PACK], F32, name="sign2")
         nc.vector.tensor_scalar(out=sign2[:], in0=g_sb[:], scalar1=0.0, scalar2=2.0, op0=ALU.is_ge, op1=ALU.mult)
+        line = keep.tile([P, 2, PACK], F32, name="line")
+        nc.vector.tensor_tensor(out=line[:], in0=ab_sb[:, :, 0:PACK], in1=g_abs[:].to_broadcast([P, 2, PACK]), op=ALU.mult)
         sign = keep.tile([P, PACK], F32, name="sign")
         nc.vector.tensor_scalar(out=sign[:], in0=sign2[:], scalar1=-1.0, scalar2=None, op0=ALU.add)
-        g_abs = keep.tile([P, PACK], F32, name="g_abs")
-        nc.vector.tensor_tensor(out=g_abs[:], in0=g_sb[:], in1=sign[:], op=ALU.mult)
         w_rep = keep.tile([P, PACK, PACK, QUAD * PACK], BF16, name="w_rep", align_bytes=64)
-        nc.vector.tensor_tensor(
-            out=w_rep[:, :, 0, :].rearrange("p e (m t) -> p e m t", t=PACK),
-            in0=w_sb[:].rearrange("p t (m e) -> p e m t", e=PACK),
-            in1=sign[:].unsqueeze(1).unsqueeze(1).to_broadcast([P, PACK, QUAD, PACK]),
-            op=ALU.mult,
-        )
-        slope = keep.tile([P, PACK], F32, name="slope")
-        nc.vector.tensor_tensor(out=slope[:], in0=a_sb[:], in1=g_abs[:], op=ALU.mult)
-        shift = keep.tile([P, PACK], F32, name="shift")
-        nc.vector.tensor_tensor(out=shift[:], in0=b_sb[:], in1=g_abs[:], op=ALU.mult)
-        nc.vector.tensor_copy(
-            out=w_rep[:, :, 1:PACK, :],
-            in_=w_rep[:, :, 0:1, :].to_broadcast([P, PACK, PACK - 1, QUAD * PACK]),
-        )
-        s32 = keep.tile([P, GROUPS, PACK], F32, name="s32")
-        nc.vector.tensor_copy(out=s32[:], in_=s_sb[:])
         w_codes = keep.tile([P, PACK, P], U32, name="w_codes", align_bytes=64)
         w_scales = keep.tile([P, PACK, P], U8, name="w_scales", align_bytes=64)
-        nc.vector.quantize_mx(
-            out=w_codes[:].rearrange("p e c -> p (e c)").bitcast(FP8X4),
-            scales=w_scales[:].rearrange("p e c -> p (e c)"),
-            in_=w_rep[:].rearrange("p e r c -> p (e r c)"),
-        )
+        s32 = keep.tile([P, GROUPS, PACK], F32, name="s32")
+
+        def sign_w():
+            nc.vector.tensor_tensor(
+                out=w_rep[:, :, 0, :].rearrange("p e (m t) -> p e m t", t=PACK),
+                in0=w_sb[:].rearrange("p t (m e) -> p e m t", e=PACK),
+                in1=sign[:].unsqueeze(1).unsqueeze(1).to_broadcast([P, PACK, QUAD, PACK]),
+                op=ALU.mult,
+            )
+
+        def repeat_w():
+            nc.vector.tensor_copy(
+                out=w_rep[:, :, 1:PACK, :],
+                in_=w_rep[:, :, 0:1, :].to_broadcast([P, PACK, PACK - 1, QUAD * PACK]),
+            )
+
+        def quantize_w():
+            nc.vector.quantize_mx(
+                out=w_codes[:].rearrange("p e c -> p (e c)").bitcast(FP8X4),
+                scales=w_scales[:].rearrange("p e c -> p (e c)"),
+                in_=w_rep[:].rearrange("p e r c -> p (e r c)"),
+            )
+
+        def pad_w():
+            nc.vector.tensor_copy(
+                out=w_pad[:, GAP:].rearrange("p (e c) -> p e c", e=PACK)[:, :, 0:QUAD].bitcast(U8),
+                in_=w_codes[:, :, 0:QUAD].bitcast(U8),
+            )
 
         v_codes = keep.tile([P, GROUPS, C], U32, name="v_codes", align_bytes=64)
         v_scales = keep.tile([P, GROUPS, C], U8, name="v_scales", align_bytes=64)
@@ -119,9 +138,10 @@ def tile_neuralbasismodelsharedshapes_kernel(tc, x, a, b, g, w, s, v_bytes, v_sc
                 src.rearrange("p t (c i) -> p c t i", i=RUN),
             )
 
-        def widen_v(q):
-            v_planes[q] = work.tile([P, PACK, C], BF16, name="v_planes", bufs=GROUPS)
-            for t in range(PACK):
+        def widen_v(q, slots=range(PACK)):
+            if q not in v_planes:
+                v_planes[q] = work.tile([P, PACK, C], BF16, name="v_planes", bufs=GROUPS)
+            for t in slots:
                 nc.scalar.activation(
                     out=v_planes[q][:, t, :], in_=v_raw[q][:, t, :].bitcast(FP8), func=ACT.Copy, scale=vs_sb[:, q, t : t + 1]
                 )
@@ -136,41 +156,60 @@ def tile_neuralbasismodelsharedshapes_kernel(tc, x, a, b, g, w, s, v_bytes, v_sc
                 out=v_codes[:, q, :].bitcast(FP8X4), scales=v_scales[:, q, :], in_=v_grouped[q][:].rearrange("p c t -> p (c t)")
             )
 
-        def affine(j, t):
+        def affine(j, t, c0, c1):
             if j not in planes:
                 planes[j] = work.tile([P, PACK, F * P], BF16, name="planes", bufs=3)
             nc.vector.tensor_scalar(
-                out=planes[j][:, t, :], in0=x_all[j][:], scalar1=slope[:, t : t + 1], scalar2=shift[:, t : t + 1], op0=ALU.mult, op1=ALU.add
+                out=planes[j][:, t, c0:c1], in0=x_all[j, c0][:], scalar1=line[:, 0, t : t + 1], scalar2=line[:, 1, t : t + 1], op0=ALU.mult, op1=ALU.add
             )
 
         def relu_views(u, c0, c1):
             j, q = divmod(u, GROUPS)
             if u not in u_grouped:
-                u_grouped[u] = work.tile([P, UNIT_COLS, PACK], BF16, name="u_grouped", bufs=4, align_bytes=64)
+                u_grouped[u] = work.tile([P, UNIT_COLS, PACK], BF16, name="u_grouped", bufs=8, align_bytes=64)
             return run_views(u_grouped[u][:, c0:c1, :], planes[j][:, :, q * UNIT_COLS + c0 : q * UNIT_COLS + c1])
 
-        def vector_share(u):
-            if u >= UNITS - 2:
-                return LAST_COLS
-            return VECTOR_COLS if u % GROUPS == 0 else 0
+        def shares(u):
+            j, q = divmod(u, GROUPS)
+            gp = GPSIMD_COLS if q == 0 and j >= 2 else (FIRST_GP if u == GROUPS else 0)
+            if j == TILES - 1:
+                return gp, LAST_COLS[q]
+            if j < 2:
+                return gp, FIRST_COLS[j] if q == GROUPS - 1 else 0
+            return gp, VECTOR_COLS if q == GROUPS - 1 else 0
 
-        def relu_scalar(u):
-            dst, src = relu_views(u, vector_share(u), UNIT_COLS)
-            nc.scalar.activation(out=dst, in_=src, func=ACT.Relu)
+        def relu_gpsimd(u):
+            gp, ve = shares(u)
+            if gp:
+                j, q = divmod(u, GROUPS)
+                relu_views(u, 0, gp)
+                nc.gpsimd.tensor_scalar(
+                    out=u_grouped[u][:, 0:gp, :],
+                    in0=planes[j][:, :, q * UNIT_COLS : q * UNIT_COLS + gp].rearrange("p t c -> p c t"),
+                    scalar1=BIG, scalar2=0.0, op0=ALU.min, op1=ALU.max,
+                )
 
         def relu_vector(u):
-            dst, src = relu_views(u, 0, vector_share(u))
-            nc.vector.tensor_scalar(out=dst, in0=src, scalar1=0.0, scalar2=None, op0=ALU.max)
+            gp, ve = shares(u)
+            if ve:
+                dst, src = relu_views(u, gp, gp + ve)
+                nc.vector.tensor_scalar(out=dst, in0=src, scalar1=0.0, scalar2=None, op0=ALU.max)
+
+        def relu_scalar(u):
+            gp, ve = shares(u)
+            if gp + ve < UNIT_COLS:
+                dst, src = relu_views(u, gp + ve, UNIT_COLS)
+                nc.scalar.activation(out=dst, in_=src, func=ACT.Relu)
 
         def quantize_u(u):
-            codes = work.tile([P, UNIT_COLS], U32, name="u_codes", bufs=3, align_bytes=64)
-            scales = work.tile([P, UNIT_COLS], U8, name="u_scales", bufs=3, align_bytes=64)
+            codes = work.tile([P, UNIT_COLS], U32, name="u_codes", bufs=4, align_bytes=64)
+            scales = work.tile([P, UNIT_COLS], U8, name="u_scales", bufs=4, align_bytes=64)
             u_mx[u] = (codes, scales)
             nc.vector.quantize_mx(out=codes[:].bitcast(FP8X4), scales=scales[:], in_=u_grouped[u][:].rearrange("p c t -> p (c t)"))
 
         def first_matmul(u):
             codes, scales = u_mx[u]
-            z_ps[u] = psum.tile([P, PACK, P], F32, name="z_ps", tag="z", bufs=4)
+            z_ps[u] = psum.tile([P, PACK, P], F32, name="z_ps", tag="z", bufs=6)
             for e in range(PACK):
                 for l in range(PACK):
                     w0 = GAP + e * P - l * QUAD
@@ -186,7 +225,7 @@ def tile_neuralbasismodelsharedshapes_kernel(tc, x, a, b, g, w, s, v_bytes, v_sc
 
         def make_q(u):
             q = u % GROUPS
-            q_grouped[u] = work.tile([P, P, PACK], BF16, name="q_grouped", bufs=3, align_bytes=64)
+            q_grouped[u] = work.tile([P, P, PACK], BF16, name="q_grouped", bufs=5, align_bytes=64)
             nc.vector.scalar_tensor_tensor(
                 out=q_grouped[u][:],
                 in0=z_ps[u][:].rearrange("p e n -> p n e"),
@@ -197,8 +236,8 @@ def tile_neuralbasismodelsharedshapes_kernel(tc, x, a, b, g, w, s, v_bytes, v_sc
             )
 
         def quantize_q(u):
-            codes = work.tile([P, P], U32, name="q_codes", bufs=3, align_bytes=64)
-            scales = work.tile([P, P], U8, name="q_scales", bufs=3, align_bytes=64)
+            codes = work.tile([P, P], U32, name="q_codes", bufs=5, align_bytes=64)
+            scales = work.tile([P, P], U8, name="q_scales", bufs=5, align_bytes=64)
             q_mx[u] = (codes, scales)
             nc.vector.quantize_mx(out=codes[:].bitcast(FP8X4), scales=scales[:], in_=q_grouped[u][:].rearrange("p n t -> p (n t)"))
 
@@ -224,40 +263,101 @@ def tile_neuralbasismodelsharedshapes_kernel(tc, x, a, b, g, w, s, v_bytes, v_sc
             nc.scalar.copy(out=result[:], in_=acc[j][:])
             nc.sync.dma_start(out=out_tiles[j], in_=result[:])
 
-        for q in range(GROUPS):
-            widen_v(q)
-        group_v(0)
-        nc.vector.tensor_copy(
-            out=w_pad[:, GAP:].rearrange("p (e c) -> p e c", e=PACK)[:, :, 0:QUAD].bitcast(U8),
-            in_=w_codes[:, :, 0:QUAD].bitcast(U8),
-        )
-        group_v(1)
-        quantize_v(0)
-        group_v(2)
-        quantize_v(1)
-        for t in range(PACK):
-            affine(0, t)
+        def first_stage(u):
+            if 0 <= u < UNITS:
+                quantize_u(u)
+                first_matmul(u)
 
-        for step in range(UNITS + 5):
-            j, q = divmod(step, GROUPS)
-            if step < UNITS:
-                relu_scalar(step)
-                if vector_share(step):
-                    relu_vector(step)
-            if step == 0:
+        def second_stage(u):
+            if 0 <= u < UNITS:
+                quantize_q(u)
+                second_matmul(u)
+
+        widen_v(0, range(1))
+        fetch_first(0)
+        widen_v(0, range(1, 2))
+        fetch_first(half)
+        widen_v(0, range(2, PACK))
+        sign_w()
+        for t in range(PACK):
+            affine(0, t, 0, half)
+        repeat_w()
+        for t in range(PACK):
+            affine(0, t, half, tile_cols)
+        relu_scalar(0)
+        widen_v(1)
+        for u in range(1, GROUPS):
+            relu_scalar(u)
+        quantize_w()
+        group_v(0)
+        pad_w()
+        nc.vector.tensor_copy(out=s32[:], in_=s_sb[:])
+        first_stage(0)
+        quantize_v(0)
+        relu_vector(3)
+        group_v(1)
+        affine(1, 0, 0, tile_cols)
+        quantize_v(1)
+        first_stage(1)
+        for t in range(1, PACK):
+            affine(1, t, 0, tile_cols)
+        relu_gpsimd(GROUPS)
+        make_q(0)
+        make_q(1)
+
+        for j in range(1, TILES - 1):
+            u0 = GROUPS * j
+            relu_scalar(u0)
+            for u in range(u0 - 6, u0 - 2):
+                second_stage(u)
+            if j == 1:
+                widen_v(2)
+            relu_scalar(u0 + 1)
+            if j >= 2:
+                store(j - 2)
+            if j == 1:
+                widen_v(3)
+            for u in range(u0 + 2, u0 + GROUPS):
+                relu_scalar(u)
+            first_stage(u0 - 2)
+            first_stage(u0 - 1)
+            affine(j + 1, 0, 0, tile_cols)
+            first_stage(u0)
+            affine(j + 1, 1, 0, tile_cols)
+            if j == 1:
+                group_v(2)
+                relu_vector(u0 + GROUPS - 1)
                 quantize_v(2)
+            affine(j + 1, 2, 0, tile_cols)
+            first_stage(u0 + 1)
+            if j == 1:
                 group_v(3)
-            if step == 1:
+            affine(j + 1, 3, 0, tile_cols)
+            if j == 1:
                 quantize_v(3)
-            if 0 <= step - 1 < UNITS:
-                quantize_u(step - 1)
-                first_matmul(step - 1)
-            if j + 1 < TILES:
-                affine(j + 1, q)
-            if 0 <= step - 3 < UNITS:
-                quantize_q(step - 3)
-                second_matmul(step - 3)
-            if 0 <= step - 2 < UNITS:
-                make_q(step - 2)
-            if step >= 7 and (step - 7) % GROUPS == 0 and (step - 7) // GROUPS < TILES:
-                store((step - 7) // GROUPS)
+            else:
+                relu_vector(u0 + GROUPS - 1)
+            relu_gpsimd(u0 + GROUPS)
+            for u in range(u0 - 2, u0 + 2):
+                make_q(u)
+
+        u0 = UNITS - GROUPS
+        relu_scalar(u0)
+        for u in range(u0 - 6, u0 - 2):
+            second_stage(u)
+        relu_scalar(u0 + 1)
+        store(TILES - 3)
+        for u in range(u0 + 2, UNITS):
+            relu_scalar(u)
+        first_stage(u0 - 2)
+        first_stage(u0 - 1)
+        for u in range(u0, UNITS):
+            relu_vector(u)
+        for u in range(u0 - 2, UNITS + 1):
+            first_stage(u + 2)
+            second_stage(u - 1 if u > u0 - 2 else -1)
+            if u - 1 == u0 - 1:
+                store(TILES - 2)
+            if u < UNITS:
+                make_q(u)
+        store(TILES - 1)

@@ -24,12 +24,14 @@ UNIT_COLS = PACK * P
 QUAD = 32
 GAP = P - QUAD
 RUN = 4
-VECTOR_COLS = 160
-LAST_COLS = (0, 0, 128, 256)
-FIRST_COLS = (512, 512)
 GPSIMD_COLS = 320
+VECTOR_COLS = 192
+HEAD_COLS = 512
+EARLY_COLS = 192
+AHEAD_FROM = 0
+LATE_COLS = 320
+LAST_COLS = (0, 0, 0)
 BIG = 3.3895313892515355e38
-FIRST_GP = 128
 
 
 def tile_neuralbasismodelsharedshapes_kernel(tc, x, a, b, g, w, s, v_bytes, v_scale, out):
@@ -40,6 +42,8 @@ def tile_neuralbasismodelsharedshapes_kernel(tc, x, a, b, g, w, s, v_bytes, v_sc
         psum = ctx.enter_context(tc.psum_pool(name="psum", bufs=1))
         ctx.enter_context(tc.manual_schedule())
 
+        ident = keep.tile([P, P], BF16, name="ident")
+        make_identity(nc, ident[:])
         x_rows = keep.tile([P, TILES * F], BF16, name="x_rows")
         nc.sync.dma_start(out=x_rows[:], in_=x.rearrange("(p j) f -> p (j f)", j=TILES))
         g_sb = keep.tile([P, PACK], BF16, name="g_sb")
@@ -54,29 +58,17 @@ def tile_neuralbasismodelsharedshapes_kernel(tc, x, a, b, g, w, s, v_bytes, v_sc
         nc.sync.dma_start(out=v_raw[0][:], in_=v_view[0])
         w_sb = keep.tile([P, PACK, K], BF16, name="w_sb")
         nc.sync.dma_start(out=w_sb[:], in_=w.rearrange("(p t) k -> p t k", t=PACK))
-        nc.sync.dma_start(out=v_raw[1][:], in_=v_view[1])
-        nc.sync.dma_start(out=v_raw[2][:], in_=v_view[2])
-        nc.sync.dma_start(out=v_raw[3][:], in_=v_view[3])
         s_sb = keep.tile([P, GROUPS, PACK], BF16, name="s_sb")
         nc.scalar.dma_start(out=s_sb[:], in_=s.rearrange("f k -> (f k)").rearrange("(q p t) -> p q t", p=P, t=PACK))
+        nc.sync.dma_start(out=v_raw[1][:], in_=v_view[1])
 
-        ident = keep.tile([P, P], BF16, name="ident")
-        make_identity(nc, ident[:])
         w_pad = keep.tile([P, GAP + PACK * P], U32, name="w_pad", align_bytes=64)
         nc.vector.memset(w_pad[:], 0)
         xt_ps = psum.tile([P, P], BF16, name="xt_ps", tag="acc", bufs=2)
         nc.tensor.transpose(xt_ps[:], x_rows[:], ident[:])
-        xt_sb = keep.tile([P, P], BF16, name="xt_sb")
-        nc.vector.tensor_copy(out=xt_sb[:], in_=xt_ps[:])
-        parked = out[0:F, :].rearrange("r c -> (r c)")
-        nc.scalar.dma_start(out=parked.rearrange("(p n) -> p n", p=P), in_=xt_sb[:].bitcast(F32))
         tile_cols = F * P
         half = tile_cols // 2
         x_all = {}
-        for j in range(1, TILES):
-            x_all[j, 0] = keep.tile([P, tile_cols], BF16, name="x_all%d" % j)
-            words = parked[j * half : (j + 1) * half]
-            nc.sync.dma_start(out=x_all[j, 0][:].bitcast(F32), in_=words.partition_broadcast(P))
         first_ps = {}
         for c0 in (0, half):
             first_ps[c0] = psum.tile([P, half], BF16, name="first_ps", tag="z", bufs=6)
@@ -95,6 +87,17 @@ def tile_neuralbasismodelsharedshapes_kernel(tc, x, a, b, g, w, s, v_bytes, v_sc
         nc.vector.tensor_tensor(out=line[:], in0=ab_sb[:, :, 0:PACK], in1=g_abs[:].to_broadcast([P, 2, PACK]), op=ALU.mult)
         sign = keep.tile([P, PACK], F32, name="sign")
         nc.vector.tensor_scalar(out=sign[:], in0=sign2[:], scalar1=-1.0, scalar2=None, op0=ALU.add)
+        xt_sb = keep.tile([P, P], BF16, name="xt_sb")
+        nc.vector.tensor_copy(out=xt_sb[:], in_=xt_ps[:])
+        parked = out[0:F, :].rearrange("r c -> (r c)")
+        nc.sync.dma_start(out=parked.rearrange("(p n) -> p n", p=P), in_=xt_sb[:].bitcast(F32))
+        for j in range(1, TILES):
+            x_all[j, 0] = keep.tile([P, tile_cols], BF16, name="x_all%d" % j)
+            words = parked[j * half : (j + 1) * half]
+            nc.sync.dma_start(out=x_all[j, 0][:].bitcast(F32), in_=words.partition_broadcast(P))
+            if j == 2:
+                nc.sync.dma_start(out=v_raw[2][:], in_=v_view[2])
+                nc.sync.dma_start(out=v_raw[3][:], in_=v_view[3])
         w_rep = keep.tile([P, PACK, PACK, QUAD * PACK], BF16, name="w_rep", align_bytes=64)
         w_codes = keep.tile([P, PACK, P], U32, name="w_codes", align_bytes=64)
         w_scales = keep.tile([P, PACK, P], U8, name="w_scales", align_bytes=64)
@@ -140,7 +143,7 @@ def tile_neuralbasismodelsharedshapes_kernel(tc, x, a, b, g, w, s, v_bytes, v_sc
 
         def widen_v(q, slots=range(PACK)):
             if q not in v_planes:
-                v_planes[q] = work.tile([P, PACK, C], BF16, name="v_planes", bufs=GROUPS)
+                v_planes[q] = work.tile([P, PACK, C], BF16, name="v_planes", bufs=2)
             for t in slots:
                 nc.scalar.activation(
                     out=v_planes[q][:, t, :], in_=v_raw[q][:, t, :].bitcast(FP8), func=ACT.Copy, scale=vs_sb[:, q, t : t + 1]
@@ -158,9 +161,9 @@ def tile_neuralbasismodelsharedshapes_kernel(tc, x, a, b, g, w, s, v_bytes, v_sc
 
         def affine(j, t, c0, c1):
             if j not in planes:
-                planes[j] = work.tile([P, PACK, F * P], BF16, name="planes", bufs=3)
+                planes[j] = work.tile([P, PACK, F * P], BF16, name="planes", bufs=4)
             nc.vector.tensor_scalar(
-                out=planes[j][:, t, c0:c1], in0=x_all[j, c0][:], scalar1=line[:, 0, t : t + 1], scalar2=line[:, 1, t : t + 1], op0=ALU.mult, op1=ALU.add
+                out=planes[j][:, t, c0:c1], in0=x_all[j, c0][:] if j == 0 else x_all[j, 0][:, c0:c1], scalar1=line[:, 0, t : t + 1], scalar2=line[:, 1, t : t + 1], op0=ALU.mult, op1=ALU.add
             )
 
         def relu_views(u, c0, c1):
@@ -171,12 +174,17 @@ def tile_neuralbasismodelsharedshapes_kernel(tc, x, a, b, g, w, s, v_bytes, v_sc
 
         def shares(u):
             j, q = divmod(u, GROUPS)
-            gp = GPSIMD_COLS if q == 0 and j >= 2 else (FIRST_GP if u == GROUPS else 0)
+            if u == 0:
+                return 0, 0
+            if q == 0:
+                return GPSIMD_COLS, VECTOR_COLS if j >= GROUPS else EARLY_COLS
             if j == TILES - 1:
-                return gp, LAST_COLS[q]
-            if j < 2:
-                return gp, FIRST_COLS[j] if q == GROUPS - 1 else 0
-            return gp, VECTOR_COLS if q == GROUPS - 1 else 0
+                return 0, LAST_COLS[q - 1]
+            if u == UNITS - GROUPS - 1:
+                return 0, LATE_COLS
+            if u == 1:
+                return 0, HEAD_COLS
+            return 0, 0
 
         def relu_gpsimd(u):
             gp, ve = shares(u)
@@ -223,55 +231,62 @@ def tile_neuralbasismodelsharedshapes_kernel(tc, x, a, b, g, w, s, v_bytes, v_sc
                         stop=(l == PACK - 1),
                     )
 
-        def make_q(u):
-            q = u % GROUPS
-            q_grouped[u] = work.tile([P, P, PACK], BF16, name="q_grouped", bufs=5, align_bytes=64)
-            nc.vector.scalar_tensor_tensor(
-                out=q_grouped[u][:],
-                in0=z_ps[u][:].rearrange("p e n -> p n e"),
-                scalar=0.0,
-                in1=s32[:, q : q + 1, :].to_broadcast([P, P, PACK]),
-                op0=ALU.max,
-                op1=ALU.mult,
-            )
+        def make_q(units):
+            batch = work.tile([P, len(units), P, PACK], BF16, name="q_grouped", bufs=4, align_bytes=64)
+            for i, u in enumerate(units):
+                q = u % GROUPS
+                q_grouped[u] = batch
+                nc.vector.scalar_tensor_tensor(
+                    out=batch[:, i, :, :],
+                    in0=z_ps[u][:].rearrange("p e n -> p n e"),
+                    scalar=0.0,
+                    in1=s32[:, q : q + 1, :].to_broadcast([P, P, PACK]),
+                    op0=ALU.max,
+                    op1=ALU.mult,
+                )
 
-        def quantize_q(u):
-            codes = work.tile([P, P], U32, name="q_codes", bufs=5, align_bytes=64)
-            scales = work.tile([P, P], U8, name="q_scales", bufs=5, align_bytes=64)
-            q_mx[u] = (codes, scales)
-            nc.vector.quantize_mx(out=codes[:].bitcast(FP8X4), scales=scales[:], in_=q_grouped[u][:].rearrange("p n t -> p (n t)"))
+        def quantize_q(units):
+            codes = work.tile([P, len(units) * P], U32, name="q_codes", bufs=5, align_bytes=64)
+            scales = work.tile([P, len(units) * P], U8, name="q_scales", bufs=5, align_bytes=64)
+            nc.vector.quantize_mx(out=codes[:].bitcast(FP8X4), scales=scales[:], in_=q_grouped[units[0]][:].rearrange("p i n t -> p (i n t)"))
+            for i, u in enumerate(units):
+                q_mx[u] = (codes[:, i * P : (i + 1) * P], scales[:, i * P : (i + 1) * P])
 
-        def second_matmul(u):
+        def second_matmul(u, first, last):
             j, q = divmod(u, GROUPS)
             codes, scales = q_mx[u]
-            if q == 0:
-                acc[j] = psum.tile([P, C], F32, name="acc", tag="acc", bufs=2)
-            nc.tensor.matmul_mx(
-                out=acc[j][:],
-                lhsT=codes[:].bitcast(FP8X4),
-                lhsT_scale=scales[:],
-                rhs=v_codes[:, q, :].bitcast(FP8X4),
-                rhs_scale=v_scales[:, q, :],
-                start=(q == 0),
-                stop=(q == GROUPS - 1),
-            )
+            if first:
+                if j < TILES - 1:
+                    acc[j] = [psum.tile([P, C], F32, name="acc", tag="acc", bufs=2)]
+                else:
+                    acc[j] = [psum.tile([P, C // 2], F32, name="acc_half", tag="z", bufs=6) for h in range(2)]
+            width = C // len(acc[j])
+            for h, part in enumerate(acc[j]):
+                nc.tensor.matmul_mx(
+                    out=part[:],
+                    lhsT=codes.bitcast(FP8X4),
+                    lhsT_scale=scales,
+                    rhs=v_codes[:, q, h * width : (h + 1) * width].bitcast(FP8X4),
+                    rhs_scale=v_scales[:, q, h * width : (h + 1) * width],
+                    start=first,
+                    stop=last,
+                )
 
         out_tiles = out.rearrange("(p j) c -> j p c", j=TILES)
 
         def store(j):
-            result = work.tile([P, C], F32, name="result", bufs=TILES)
-            nc.scalar.copy(out=result[:], in_=acc[j][:])
+            result = work.tile([P, C], F32, name="result", bufs=4)
+            nc.scalar.copy(out=result[:], in_=acc[j][0][:])
             nc.sync.dma_start(out=out_tiles[j], in_=result[:])
 
         def first_stage(u):
-            if 0 <= u < UNITS:
-                quantize_u(u)
-                first_matmul(u)
+            quantize_u(u)
+            first_matmul(u)
 
-        def second_stage(u):
-            if 0 <= u < UNITS:
-                quantize_q(u)
-                second_matmul(u)
+        def second_stage(units):
+            quantize_q(units)
+            for u in units:
+                second_matmul(u, u == units[0], u == units[-1])
 
         widen_v(0, range(1))
         fetch_first(0)
@@ -279,85 +294,96 @@ def tile_neuralbasismodelsharedshapes_kernel(tc, x, a, b, g, w, s, v_bytes, v_sc
         fetch_first(half)
         widen_v(0, range(2, PACK))
         sign_w()
-        for t in range(PACK):
-            affine(0, t, 0, half)
         repeat_w()
         for t in range(PACK):
+            affine(0, t, 0, half)
+        for t in range(PACK):
             affine(0, t, half, tile_cols)
+        def tile_units(j):
+            return list(range(GROUPS * j, GROUPS * (j + 1)))
+
         relu_scalar(0)
-        widen_v(1)
-        for u in range(1, GROUPS):
-            relu_scalar(u)
         quantize_w()
         group_v(0)
         pad_w()
         nc.vector.tensor_copy(out=s32[:], in_=s_sb[:])
-        first_stage(0)
         quantize_v(0)
-        relu_vector(3)
-        group_v(1)
-        affine(1, 0, 0, tile_cols)
-        quantize_v(1)
-        first_stage(1)
-        for t in range(1, PACK):
-            affine(1, t, 0, tile_cols)
-        relu_gpsimd(GROUPS)
-        make_q(0)
-        make_q(1)
 
-        for j in range(1, TILES - 1):
+        def affine_step(j, t):
+            if j < TILES:
+                affine(j, t, GPSIMD_COLS if t == PACK - 1 else 0, tile_cols)
+
+        for j in range(TILES - 1):
             u0 = GROUPS * j
-            relu_scalar(u0)
-            for u in range(u0 - 6, u0 - 2):
-                second_stage(u)
-            if j == 1:
-                widen_v(2)
+            v_pass = j + 1 if j + 1 < GROUPS else None
             relu_scalar(u0 + 1)
-            if j >= 2:
+            if v_pass:
+                widen_v(v_pass)
+            if j > 0:
+                relu_scalar(u0)
+            relu_scalar(u0 + 2)
+            relu_scalar(u0 + 3)
+            if j == GROUPS - 1:
+                store(0)
+            if j >= GROUPS - 1:
                 store(j - 2)
-            if j == 1:
-                widen_v(3)
-            for u in range(u0 + 2, u0 + GROUPS):
-                relu_scalar(u)
-            first_stage(u0 - 2)
-            first_stage(u0 - 1)
-            affine(j + 1, 0, 0, tile_cols)
-            first_stage(u0)
-            affine(j + 1, 1, 0, tile_cols)
-            if j == 1:
-                group_v(2)
-                relu_vector(u0 + GROUPS - 1)
-                quantize_v(2)
-            affine(j + 1, 2, 0, tile_cols)
-            first_stage(u0 + 1)
-            if j == 1:
-                group_v(3)
-            affine(j + 1, 3, 0, tile_cols)
-            if j == 1:
-                quantize_v(3)
-            else:
-                relu_vector(u0 + GROUPS - 1)
+            own, other = (u0, u0 + 1) if j > 0 else (u0 + 1, u0)
+            ahead = j + 2 if j >= AHEAD_FROM else j + 1
+            relu_vector(own)
+            first_stage(other)
+            first_stage(own)
+            if v_pass:
+                group_v(v_pass)
+            if j == AHEAD_FROM:
+                for t in range(PACK):
+                    affine_step(j + 1, t)
+            relu_vector(u0 + 3)
+            first_stage(u0 + 2)
+            if v_pass:
+                quantize_v(v_pass)
+            affine_step(ahead, 0)
+            affine_step(ahead, 1)
+            affine_step(ahead, 2)
+            first_stage(u0 + 3)
+            affine_step(ahead, 3)
+            if j == TILES - 2:
+                relu_scalar(u0 + GROUPS + 1)
+                first_stage(u0 + GROUPS + 1)
+            affine(j + 1, 3, 0, GPSIMD_COLS)
+            if j == 2:
+                second_stage(tile_units(0))
+            if j >= 2:
+                second_stage(tile_units(j - 1))
             relu_gpsimd(u0 + GROUPS)
-            for u in range(u0 - 2, u0 + 2):
-                make_q(u)
+            make_q(tile_units(j))
 
-        u0 = UNITS - GROUPS
-        relu_scalar(u0)
-        for u in range(u0 - 6, u0 - 2):
-            second_stage(u)
-        relu_scalar(u0 + 1)
-        store(TILES - 3)
-        for u in range(u0 + 2, UNITS):
+        j = TILES - 1
+        u0 = GROUPS * j
+        order = (u0 + 1, u0 + 2, u0, u0 + 3)
+        for u in order[1:]:
             relu_scalar(u)
-        first_stage(u0 - 2)
-        first_stage(u0 - 1)
-        for u in range(u0, UNITS):
-            relu_vector(u)
-        for u in range(u0 - 2, UNITS + 1):
-            first_stage(u + 2)
-            second_stage(u - 1 if u > u0 - 2 else -1)
-            if u - 1 == u0 - 1:
-                store(TILES - 2)
-            if u < UNITS:
-                make_q(u)
-        store(TILES - 1)
+        store(j - 2)
+        relu_vector(u0)
+        first_stage(order[1])
+        relu_vector(u0 + 3)
+        first_stage(order[2])
+        make_q([order[0]])
+        first_stage(order[3])
+        quantize_q(tile_units(j - 1))
+        make_q([order[1]])
+        for u in tile_units(j - 1):
+            second_matmul(u, u == u0 - GROUPS, u == u0 - 1)
+        store(j - 1)
+        quantize_q([order[0]])
+        make_q([order[2]])
+        quantize_q([order[1]])
+        make_q([order[3]])
+        quantize_q([order[2]])
+        quantize_q([order[3]])
+        for u in order:
+            second_matmul(u, u == order[0], u == order[-1])
+        halves = [work.tile([P, C // 2], F32, name="half%d" % h, bufs=1) for h in range(2)]
+        nc.vector.tensor_copy(out=halves[0][:], in_=acc[j][0][:])
+        nc.scalar.copy(out=halves[1][:], in_=acc[j][1][:])
+        nc.sync.dma_start(out=out_tiles[j][:, 0 : C // 2], in_=halves[0][:])
+        nc.scalar.dma_start(out=out_tiles[j][:, C // 2 : C], in_=halves[1][:])

@@ -24,12 +24,12 @@ UNIT_COLS = PACK * P
 QUAD = 32
 GAP = P - QUAD
 RUN = 4
-GPSIMD_COLS = 320
-VECTOR_COLS = 192
+GPSIMD_COLS = 384
+VECTOR_COLS = 128
 HEAD_COLS = 512
-EARLY_COLS = 192
+EARLY_COLS = 128
 AHEAD_FROM = 0
-LATE_COLS = 320
+LATE_COLS = 448
 LAST_COLS = (0, 0, 0)
 BIG = 3.3895313892515355e38
 

from contextlib import ExitStack

import concourse.mybir as mybir
from concourse.masks import make_identity

N, F, H, K, C = 1024, 16, 512, 128, 512
FLOPS = 2 * N * F * H * K + 2 * N * F * K * C

F32 = mybir.dt.float32
BF16 = mybir.dt.bfloat16
U32 = mybir.dt.uint32
U8 = mybir.dt.uint8
FP8 = mybir.dt.float8_e4m3fn
FP8X4 = mybir.dt.float8_e4m3fn_x4
ALU = mybir.AluOpType
ACT = mybir.ActivationFunctionType

P = 128
PACK = 4
TILES = N // P
GROUPS = F // PACK
UNITS = TILES * GROUPS
UNIT_COLS = PACK * P
QUAD = 32
GAP = P - QUAD
RUN = 4
GPSIMD_COLS = 384
VECTOR_COLS = 128
HEAD_COLS = 512
EARLY_COLS = 128
AHEAD_FROM = 0
LATE_COLS = 448
LAST_COLS = (0, 0, 0)
BIG = 3.3895313892515355e38


def tile_neuralbasismodelsharedshapes_kernel(tc, x, a, b, g, w, s, v_bytes, v_scale, out):
    nc = tc.nc
    with ExitStack() as ctx:
        keep = ctx.enter_context(tc.tile_pool(name="keep", bufs=1))
        work = ctx.enter_context(tc.tile_pool(name="work", bufs=2))
        psum = ctx.enter_context(tc.psum_pool(name="psum", bufs=1))
        ctx.enter_context(tc.manual_schedule())

        ident = keep.tile([P, P], BF16, name="ident")
        make_identity(nc, ident[:])
        x_rows = keep.tile([P, TILES * F], BF16, name="x_rows")
        nc.sync.dma_start(out=x_rows[:], in_=x.rearrange("(p j) f -> p (j f)", j=TILES))
        g_sb = keep.tile([P, PACK], BF16, name="g_sb")
        ab_sb = keep.tile([P, 2, 16], BF16, name="ab_sb")
        nc.scalar.dma_start(out=g_sb[:], in_=g.rearrange("(p t) -> p t", t=PACK))
        nc.scalar.dma_start(out=ab_sb[:, 0, 0:PACK], in_=a.rearrange("(p t) -> p t", t=PACK))
        nc.scalar.dma_start(out=ab_sb[:, 1, 0:PACK], in_=b.rearrange("(p t) -> p t", t=PACK))
        vs_sb = keep.tile([P, GROUPS, PACK], F32, name="vs_sb")
        nc.sync.dma_start(out=vs_sb[:], in_=v_scale.rearrange("(q p t) o -> p q (t o)", p=P, t=PACK))
        v_view = v_bytes.rearrange("(q p t) c -> q p t c", p=P, t=PACK)
        v_raw = [keep.tile([P, PACK, C], U8, name="v_raw%d" % q) for q in range(GROUPS)]
        nc.sync.dma_start(out=v_raw[0][:], in_=v_view[0])
        w_sb = keep.tile([P, PACK, K], BF16, name="w_sb")
        nc.sync.dma_start(out=w_sb[:], in_=w.rearrange("(p t) k -> p t k", t=PACK))
        s_sb = keep.tile([P, GROUPS, PACK], BF16, name="s_sb")
        nc.scalar.dma_start(out=s_sb[:], in_=s.rearrange("f k -> (f k)").rearrange("(q p t) -> p q t", p=P, t=PACK))
        nc.sync.dma_start(out=v_raw[1][:], in_=v_view[1])

        w_pad = keep.tile([P, GAP + PACK * P], U32, name="w_pad", align_bytes=64)
        nc.vector.memset(w_pad[:], 0)
        xt_ps = psum.tile([P, P], BF16, name="xt_ps", tag="acc", bufs=2)
        nc.tensor.transpose(xt_ps[:], x_rows[:], ident[:])
        tile_cols = F * P
        half = tile_cols // 2
        x_all = {}
        first_ps = {}
        for c0 in (0, half):
            first_ps[c0] = psum.tile([P, half], BF16, name="first_ps", tag="z", bufs=6)
            for f in range(c0 // P, (c0 + half) // P):
                nc.tensor.transpose(first_ps[c0][:, f * P - c0 : (f + 1) * P - c0], x_rows[:, f : f + 1].to_broadcast([P, P]), ident[:])

        def fetch_first(c0):
            x_all[0, c0] = keep.tile([P, half], BF16, name="x_first%d" % c0)
            nc.scalar.copy(out=x_all[0, c0][:], in_=first_ps[c0][:])

        g_abs = keep.tile([P, 1, PACK], F32, name="g_abs")
        nc.vector.scalar_tensor_tensor(out=g_abs[:, 0, :], in0=g_sb[:], scalar=-1.0, in1=g_sb[:], op0=ALU.mult, op1=ALU.max)
        sign2 = keep.tile([P, PACK], F32, name="sign2")
        nc.vector.tensor_scalar(out=sign2[:], in0=g_sb[:], scalar1=0.0, scalar2=2.0, op0=ALU.is_ge, op1=ALU.mult)
        line = keep.tile([P, 2, PACK], F32, name="line")
        nc.vector.tensor_tensor(out=line[:], in0=ab_sb[:, :, 0:PACK], in1=g_abs[:].to_broadcast([P, 2, PACK]), op=ALU.mult)
        sign = keep.tile([P, PACK], F32, name="sign")
        nc.vector.tensor_scalar(out=sign[:], in0=sign2[:], scalar1=-1.0, scalar2=None, op0=ALU.add)
        xt_sb = keep.tile([P, P], BF16, name="xt_sb")
        nc.vector.tensor_copy(out=xt_sb[:], in_=xt_ps[:])
        parked = out[0:F, :].rearrange("r c -> (r c)")
        nc.sync.dma_start(out=parked.rearrange("(p n) -> p n", p=P), in_=xt_sb[:].bitcast(F32))
        for j in range(1, TILES):
            x_all[j, 0] = keep.tile([P, tile_cols], BF16, name="x_all%d" % j)
            words = parked[j * half : (j + 1) * half]
            nc.sync.dma_start(out=x_all[j, 0][:].bitcast(F32), in_=words.partition_broadcast(P))
            if j == 2:
                nc.sync.dma_start(out=v_raw[2][:], in_=v_view[2])
                nc.sync.dma_start(out=v_raw[3][:], in_=v_view[3])
        w_rep = keep.tile([P, PACK, PACK, QUAD * PACK], BF16, name="w_rep", align_bytes=64)
        w_codes = keep.tile([P, PACK, P], U32, name="w_codes", align_bytes=64)
        w_scales = keep.tile([P, PACK, P], U8, name="w_scales", align_bytes=64)
        s32 = keep.tile([P, GROUPS, PACK], F32, name="s32")

        def sign_w():
            nc.vector.tensor_tensor(
                out=w_rep[:, :, 0, :].rearrange("p e (m t) -> p e m t", t=PACK),
                in0=w_sb[:].rearrange("p t (m e) -> p e m t", e=PACK),
                in1=sign[:].unsqueeze(1).unsqueeze(1).to_broadcast([P, PACK, QUAD, PACK]),
                op=ALU.mult,
            )

        def repeat_w():
            nc.vector.tensor_copy(
                out=w_rep[:, :, 1:PACK, :],
                in_=w_rep[:, :, 0:1, :].to_broadcast([P, PACK, PACK - 1, QUAD * PACK]),
            )

        def quantize_w():
            nc.vector.quantize_mx(
                out=w_codes[:].rearrange("p e c -> p (e c)").bitcast(FP8X4),
                scales=w_scales[:].rearrange("p e c -> p (e c)"),
                in_=w_rep[:].rearrange("p e r c -> p (e r c)"),
            )

        def pad_w():
            nc.vector.tensor_copy(
                out=w_pad[:, GAP:].rearrange("p (e c) -> p e c", e=PACK)[:, :, 0:QUAD].bitcast(U8),
                in_=w_codes[:, :, 0:QUAD].bitcast(U8),
            )

        v_codes = keep.tile([P, GROUPS, C], U32, name="v_codes", align_bytes=64)
        v_scales = keep.tile([P, GROUPS, C], U8, name="v_scales", align_bytes=64)
        v_planes, v_grouped = {}, {}
        planes, u_grouped, u_mx, z_ps, q_grouped, q_mx, acc = {}, {}, {}, {}, {}, {}, {}

        def run_views(dst, src):
            return (
                dst.rearrange("p (c i) t -> p c t i", i=RUN),
                src.rearrange("p t (c i) -> p c t i", i=RUN),
            )

        def widen_v(q, slots=range(PACK)):
            if q not in v_planes:
                v_planes[q] = work.tile([P, PACK, C], BF16, name="v_planes", bufs=2)
            for t in slots:
                nc.scalar.activation(
                    out=v_planes[q][:, t, :], in_=v_raw[q][:, t, :].bitcast(FP8), func=ACT.Copy, scale=vs_sb[:, q, t : t + 1]
                )

        def group_v(q):
            v_grouped[q] = work.tile([P, C, PACK], BF16, name="v_grouped", align_bytes=64)
            dst, src = run_views(v_grouped[q][:], v_planes[q][:])
            nc.vector.tensor_copy(out=dst, in_=src)

        def quantize_v(q):
            nc.vector.quantize_mx(
                out=v_codes[:, q, :].bitcast(FP8X4), scales=v_scales[:, q, :], in_=v_grouped[q][:].rearrange("p c t -> p (c t)")
            )

        def affine(j, t, c0, c1):
            if j not in planes:
                planes[j] = work.tile([P, PACK, F * P], BF16, name="planes", bufs=4)
            nc.vector.tensor_scalar(
                out=planes[j][:, t, c0:c1], in0=x_all[j, c0][:] if j == 0 else x_all[j, 0][:, c0:c1], scalar1=line[:, 0, t : t + 1], scalar2=line[:, 1, t : t + 1], op0=ALU.mult, op1=ALU.add
            )

        def relu_views(u, c0, c1):
            j, q = divmod(u, GROUPS)
            if u not in u_grouped:
                u_grouped[u] = work.tile([P, UNIT_COLS, PACK], BF16, name="u_grouped", bufs=8, align_bytes=64)
            return run_views(u_grouped[u][:, c0:c1, :], planes[j][:, :, q * UNIT_COLS + c0 : q * UNIT_COLS + c1])

        def shares(u):
            j, q = divmod(u, GROUPS)
            if u == 0:
                return 0, 0
            if q == 0:
                return GPSIMD_COLS, VECTOR_COLS if j >= GROUPS else EARLY_COLS
            if j == TILES - 1:
                return 0, LAST_COLS[q - 1]
            if u == UNITS - GROUPS - 1:
                return 0, LATE_COLS
            if u == 1:
                return 0, HEAD_COLS
            return 0, 0

        def relu_gpsimd(u):
            gp, ve = shares(u)
            if gp:
                j, q = divmod(u, GROUPS)
                relu_views(u, 0, gp)
                nc.gpsimd.tensor_scalar(
                    out=u_grouped[u][:, 0:gp, :],
                    in0=planes[j][:, :, q * UNIT_COLS : q * UNIT_COLS + gp].rearrange("p t c -> p c t"),
                    scalar1=BIG, scalar2=0.0, op0=ALU.min, op1=ALU.max,
                )

        def relu_vector(u):
            gp, ve = shares(u)
            if ve:
                dst, src = relu_views(u, gp, gp + ve)
                nc.vector.tensor_scalar(out=dst, in0=src, scalar1=0.0, scalar2=None, op0=ALU.max)

        def relu_scalar(u):
            gp, ve = shares(u)
            if gp + ve < UNIT_COLS:
                dst, src = relu_views(u, gp + ve, UNIT_COLS)
                nc.scalar.activation(out=dst, in_=src, func=ACT.Relu)

        def quantize_u(u):
            codes = work.tile([P, UNIT_COLS], U32, name="u_codes", bufs=4, align_bytes=64)
            scales = work.tile([P, UNIT_COLS], U8, name="u_scales", bufs=4, align_bytes=64)
            u_mx[u] = (codes, scales)
            nc.vector.quantize_mx(out=codes[:].bitcast(FP8X4), scales=scales[:], in_=u_grouped[u][:].rearrange("p c t -> p (c t)"))

        def first_matmul(u):
            codes, scales = u_mx[u]
            z_ps[u] = psum.tile([P, PACK, P], F32, name="z_ps", tag="z", bufs=6)
            for e in range(PACK):
                for l in range(PACK):
                    w0 = GAP + e * P - l * QUAD
                    nc.tensor.matmul_mx(
                        out=z_ps[u][:, e, :],
                        lhsT=w_pad[:, w0 : w0 + P].bitcast(FP8X4),
                        lhsT_scale=w_scales[:, e, :],
                        rhs=codes[:, l * P : (l + 1) * P].bitcast(FP8X4),
                        rhs_scale=scales[:, l * P : (l + 1) * P],
                        start=(l == 0),
                        stop=(l == PACK - 1),
                    )

        def make_q(units):
            batch = work.tile([P, len(units), P, PACK], BF16, name="q_grouped", bufs=4, align_bytes=64)
            for i, u in enumerate(units):
                q = u % GROUPS
                q_grouped[u] = batch
                nc.vector.scalar_tensor_tensor(
                    out=batch[:, i, :, :],
                    in0=z_ps[u][:].rearrange("p e n -> p n e"),
                    scalar=0.0,
                    in1=s32[:, q : q + 1, :].to_broadcast([P, P, PACK]),
                    op0=ALU.max,
                    op1=ALU.mult,
                )

        def quantize_q(units):
            codes = work.tile([P, len(units) * P], U32, name="q_codes", bufs=5, align_bytes=64)
            scales = work.tile([P, len(units) * P], U8, name="q_scales", bufs=5, align_bytes=64)
            nc.vector.quantize_mx(out=codes[:].bitcast(FP8X4), scales=scales[:], in_=q_grouped[units[0]][:].rearrange("p i n t -> p (i n t)"))
            for i, u in enumerate(units):
                q_mx[u] = (codes[:, i * P : (i + 1) * P], scales[:, i * P : (i + 1) * P])

        def second_matmul(u, first, last):
            j, q = divmod(u, GROUPS)
            codes, scales = q_mx[u]
            if first:
                if j < TILES - 1:
                    acc[j] = [psum.tile([P, C], F32, name="acc", tag="acc", bufs=2)]
                else:
                    acc[j] = [psum.tile([P, C // 2], F32, name="acc_half", tag="z", bufs=6) for h in range(2)]
            width = C // len(acc[j])
            for h, part in enumerate(acc[j]):
                nc.tensor.matmul_mx(
                    out=part[:],
                    lhsT=codes.bitcast(FP8X4),
                    lhsT_scale=scales,
                    rhs=v_codes[:, q, h * width : (h + 1) * width].bitcast(FP8X4),
                    rhs_scale=v_scales[:, q, h * width : (h + 1) * width],
                    start=first,
                    stop=last,
                )

        out_tiles = out.rearrange("(p j) c -> j p c", j=TILES)

        def store(j):
            result = work.tile([P, C], F32, name="result", bufs=4)
            nc.scalar.copy(out=result[:], in_=acc[j][0][:])
            nc.sync.dma_start(out=out_tiles[j], in_=result[:])

        def first_stage(u):
            quantize_u(u)
            first_matmul(u)

        def second_stage(units):
            quantize_q(units)
            for u in units:
                second_matmul(u, u == units[0], u == units[-1])

        widen_v(0, range(1))
        fetch_first(0)
        widen_v(0, range(1, 2))
        fetch_first(half)
        widen_v(0, range(2, PACK))
        sign_w()
        repeat_w()
        for t in range(PACK):
            affine(0, t, 0, half)
        for t in range(PACK):
            affine(0, t, half, tile_cols)
        def tile_units(j):
            return list(range(GROUPS * j, GROUPS * (j + 1)))

        relu_scalar(0)
        quantize_w()
        group_v(0)
        pad_w()
        nc.vector.tensor_copy(out=s32[:], in_=s_sb[:])
        quantize_v(0)

        def affine_step(j, t):
            if j < TILES:
                affine(j, t, GPSIMD_COLS if t == PACK - 1 else 0, tile_cols)

        for j in range(TILES - 1):
            u0 = GROUPS * j
            v_pass = j + 1 if j + 1 < GROUPS else None
            relu_scalar(u0 + 1)
            if v_pass:
                widen_v(v_pass)
            if j > 0:
                relu_scalar(u0)
            relu_scalar(u0 + 2)
            relu_scalar(u0 + 3)
            if j == GROUPS - 1:
                store(0)
            if j >= GROUPS - 1:
                store(j - 2)
            own, other = (u0, u0 + 1) if j > 0 else (u0 + 1, u0)
            ahead = j + 2 if j >= AHEAD_FROM else j + 1
            relu_vector(own)
            first_stage(other)
            first_stage(own)
            if v_pass:
                group_v(v_pass)
            if j == AHEAD_FROM:
                for t in range(PACK):
                    affine_step(j + 1, t)
            relu_vector(u0 + 3)
            first_stage(u0 + 2)
            if v_pass:
                quantize_v(v_pass)
            affine_step(ahead, 0)
            affine_step(ahead, 1)
            affine_step(ahead, 2)
            first_stage(u0 + 3)
            affine_step(ahead, 3)
            if j == TILES - 2:
                relu_scalar(u0 + GROUPS + 1)
                first_stage(u0 + GROUPS + 1)
            affine(j + 1, 3, 0, GPSIMD_COLS)
            if j == 2:
                second_stage(tile_units(0))
            if j >= 2:
                second_stage(tile_units(j - 1))
            relu_gpsimd(u0 + GROUPS)
            make_q(tile_units(j))

        j = TILES - 1
        u0 = GROUPS * j
        order = (u0 + 1, u0 + 2, u0, u0 + 3)
        for u in order[1:]:
            relu_scalar(u)
        store(j - 2)
        relu_vector(u0)
        first_stage(order[1])
        relu_vector(u0 + 3)
        first_stage(order[2])
        make_q([order[0]])
        first_stage(order[3])
        quantize_q(tile_units(j - 1))
        make_q([order[1]])
        for u in tile_units(j - 1):
            second_matmul(u, u == u0 - GROUPS, u == u0 - 1)
        store(j - 1)
        quantize_q([order[0]])
        make_q([order[2]])
        quantize_q([order[1]])
        make_q([order[3]])
        quantize_q([order[2]])
        quantize_q([order[3]])
        for u in order:
            second_matmul(u, u == order[0], u == order[-1])
        halves = [work.tile([P, C // 2], F32, name="half%d" % h, bufs=1) for h in range(2)]
        nc.vector.tensor_copy(out=halves[0][:], in_=acc[j][0][:])
        nc.scalar.copy(out=halves[1][:], in_=acc[j][1][:])
        nc.sync.dma_start(out=out_tiles[j][:, 0 : C // 2], in_=halves[0][:])
        nc.scalar.dma_start(out=out_tiles[j][:, C // 2 : C], in_=halves[1][:])
